import numpy as np, ml_dtypes
CORES = [6,15,38,47]
N = 4
import mx_ref
BF = ml_dtypes.bfloat16
def entries(a):
    return np.ascontiguousarray(a.T).reshape(-1)
def table(e):
    return np.ascontiguousarray(np.reshape(e, (-1, 16)).T).astype(np.int32)
def gpick(z, e):
    return np.concatenate([z[16 * g:16 * g + 16][:, e[g]] for g in range(8)])
def tile(rs):
    return np.stack(rs, axis=2).reshape(128, -1).astype(BF)
def cut(t, i, w=512):
    return t[:, w * i:w * i + w]
def f(rng, *shape):
    return mx_ref.flush((rng.standard_normal(shape, dtype=np.float32) * np.exp2(rng.integers(-2, 3, shape[:-1] + (1,)))).astype(BF))
def wide(rng, *shape, cols=0):
    v = rng.standard_normal(shape, dtype=np.float32) * np.exp2(rng.integers(-12, 13, shape)).astype(np.float32)
    if cols: v *= np.repeat(np.exp2(rng.integers(-cols, cols + 1, shape[:-2] + (1, shape[-1] // 4))) * (rng.random(shape[:-2] + (1, shape[-1] // 4)) > 0.0625), 4, axis=-1).astype(np.float32)
    return mx_ref.flush(v.astype(BF))
TQ, O = 128, 2
def lay(k, q):
    return {"kp": np.repeat(k, 16, axis=1).astype(np.int32), "qp": np.stack([table(e) for e in q])}
def setup_inputs(rng):
    d = {"qx": f(rng, N, 128, 4 * TQ), "ky": f(rng, N, 128, 2048), "rt": np.repeat(f(rng, 1, 128, 1024), N, axis=0), "vv": f(rng, N, 128, 512 * O)}
    a = rng.integers(0, 3585)
    k = a + rng.integers(0, 512, (N, 8, 4))
    q = np.where(rng.random((N, TQ)) < 0.25, rng.integers(0, 4096, (N, TQ)), a + rng.integers(0, 512, (N, TQ)))
    return {**d, **lay(k, q)}
def setup_inputs_far(rng):
    d = setup_inputs(rng)
    k = rng.integers(1500, 2501, (N, 32)); q = np.zeros((N, TQ), int); a = int(rng.integers(0, 2))
    for r in range(N):
        k[r, rng.permutation(32)[:2]] = [1500, 2500]
        lo, hi = (2628, 4095) if (r + a) % 2 else (0, 1371)
        q[r] = rng.integers(lo, hi + 1, TQ)
        q[r, rng.permutation(TQ)[:2]] = [lo, hi]
    return {**d, **lay(k.reshape(N, 8, 4), q)}
def setup_inputs_same(rng):
    d = setup_inputs(rng); a = int(rng.integers(0, 4096))
    return {**d, **lay(np.full((N, 8, 4), a), np.full((N, TQ), a))}
def setup_inputs_descending(rng):
    d = setup_inputs(rng); a = rng.integers(0, 3585)
    q = np.stack([a + np.sort(rng.permutation(512)[:TQ])[::-1] for r in range(N)])
    k = np.stack([a + 16 * rng.permutation(32) + rng.integers(0, 16, 32) for r in range(N)])
    return {**d, **lay(k.reshape(N, 8, 4), q)}
def setup_inputs_near(rng):
    d = setup_inputs(rng); a = rng.integers(2049, 3968)
    q = np.stack([a + rng.permutation(TQ) % 128 for r in range(N)])
    k = np.stack([a + rng.permutation(np.concatenate([[0, 128], 1 + rng.permutation(127)[:30]])) for r in range(N)])
    return {**d, **lay(k.reshape(N, 8, 4), q)}
def setup_inputs_spread(rng):
    d = setup_inputs(rng); d["qx"] = wide(rng, N, 128, 4 * TQ, cols=4); return d
def check_inputs(d):
    b = []
    for r in range(N):
        k, q = d["kp"][r], entries(d["qp"][r])
        if d["rt"][r].tobytes() != d["rt"][0].tobytes(): b.append("rt")
        if k.min() < 0 or k.max() > 4095 or (k != np.repeat(k[::16], 16, axis=0)).any(): b.append("kp")
        if q.min() < 0 or q.max() > 4095: b.append("qp")
    return b
def reference(qx, ky, rt, vv, kp, qp):
    y = np.zeros((N, 128, O * TQ), np.float32)
    X = [mx_ref.quantize(qx[r]) for r in range(N)]
    for s in range(N):
        K = [mx_ref.quantize(np.ascontiguousarray(cut(ky[s], b))) for b in range(4)]
        V = [mx_ref.quantize(np.ascontiguousarray(cut(vv[s], o))) for o in range(O)]
        R = mx_ref.quantize(rt[s])
        P = [mx_ref.matmul(K[b], R) for b in range(4)]
        for r in range(N):
            A = []
            for b in range(4):
                c = np.clip(entries(qp[r])[None, :] - kp[s][::16, b][:, None], -128, 127) + 128
                A.append(np.maximum(mx_ref.matmul(K[b], X[r]) + gpick(P[b], c), np.float32(0)) * np.float32(0.03125))
            A = mx_ref.quantize(tile(A))
            for o in range(O): y[r][:, TQ * o:TQ * o + TQ] += mx_ref.matmul(V[o], A)
    return {"y": y}

@@ -1,0 +1,253 @@
+from concourse.bass import DstId, RemoteDMATransfer
+from concourse.mybir import dt, AluOpType, ActivationFunctionType
+
+F, B, I32, U16 = "float32", "bfloat16", "int32", "uint16"
+C8, U8 = "float8_e4m3fn_x4", "uint8"
+SCRATCH = {
+    "xb": ("sbuf", [128, 512], B), "kb": ("sbuf", [128, 2048], B), "rb": ("sbuf", [128, 1024], B), "vb": ("sbuf", [128, 1024], B),
+    "kpi": ("sbuf", [128, 4], I32), "kpf": ("sbuf", [128, 4], F), "qpo": ("sbuf", [128, 8], I32),
+    "xq": ("sbuf", [128, 128], C8), "xs": ("sbuf", [128, 128], U8), "kq": ("sbuf", [128, 512], C8), "ks": ("sbuf", [128, 512], U8),
+    "rq": ("sbuf", [128, 256], C8), "rs": ("sbuf", [128, 256], U8), "vq": ("sbuf", [128, 256], C8), "vs": ("sbuf", [128, 256], U8),
+    "qpl": ("sbuf", [128, 24], I32), "xlq": ("sbuf", [128, 384], C8), "xls": ("sbuf", [128, 384], U8),
+    "vlq": ("sbuf", [128, 768], C8), "vls": ("sbuf", [128, 768], U8), "alq": ("sbuf", [128, 384], C8), "als": ("sbuf", [128, 384], U8),
+    "hq": ("sbuf", [128, 128], C8), "hs": ("sbuf", [128, 128], U8),
+    "dr": ("sbuf", [128, 96], F), "offr": ("sbuf", [128, 96], U16), "do": ("sbuf", [128, 32], F), "offo": ("sbuf", [128, 32], U16),
+    "pw": ("sbuf", [128, 1024], F), "gr": ("sbuf", [128, 1536], F), "go": ("sbuf", [128, 512], F),
+    "u": ("sbuf", [128, 2048], F), "h0": ("sbuf", [128, 512], B), "h1": ("sbuf", [128, 512], B), "h2": ("sbuf", [128, 512], B), "h3": ("sbuf", [128, 512], B),
+    "aq": ("sbuf", [128, 512], C8), "as_": ("sbuf", [128, 512], U8),
+    "yb": ("sbuf", [128, 256], F),
+    "ps": ("psum", [128, 4096], F),
+}
+SEMAPHORES = (["ldx", "ldv", "ldr", "ldk0", "ldk1", "ldkp", "ldqp", "qx", "qv", "qr", "qk0", "qk1", "kpf", "d1", "d1o", "offr", "offo",
+               "qpa", "vh", "sent", "yc", "st"]
+              + [n + str(b) for n in ("p", "pc", "g", "go", "xa", "va", "aa", "rl", "qa") for b in range(4)]
+              + [n + "%d%d" % (k, b) for n in ("s", "ad") for k in range(4) for b in range(4)] + ["y0", "y1"])
+
+
+def bits(engines):
+    return sum(1 << e for e in engines)
+
+
+def peers_of(rank, T, topo):
+    me = topo.chip(T.cores[rank])
+
+    def relation(r):
+        c = topo.chip(T.cores[r])
+        return 1 if topo.mates(me, c) else 2 if topo.same_plane(me, c) else 0
+    return sorted((r for r in range(len(T.cores)) if r != rank), key=relation)
+
+
+def helpers_of(rank, T, topo):
+    me = T.cores[rank]
+    far = [T.cores[r] for r in range(len(T.cores)) if r != rank]
+    return [c for c in topo.cores_of(me) if topo.die(c) != topo.die(me) and all(topo.may_write(c, d) for d in far)][:2]
+
+
+def ids(cores, topo):
+    a = [topo.addr(c) for c in cores]
+    return [DstId(rid=x[0], pnc=x[1]) for x in a]
+
+
+def cast(g, topo, src_core, cores, src, dsts, remote_sem, local_sem):
+    eng = [e for e in topo.engines(src_core, cores[0]) if all(e in topo.engines(src_core, c) for c in cores)]
+    g.remote_dma_fused([RemoteDMATransfer(dst_ids=ids(cores, topo), dma_engine_mask=bits(eng), remote_sem=remote_sem,
+                                          srcs=[src], dsts=dsts, alu_op=0)], local_sem=local_sem)
+    return len(eng)
+
+
+def u8(v):
+    return v.bitcast(dt.uint8)
+
+
+def helper_program(g, core, T, topo, rank, o):
+    s = T.sem
+    cores = [T.cores[r] for r in peers_of(rank, T, topo)]
+    g.wait_ge(s.vh, 8)
+    n = cast(g, topo, core, cores, u8(T.hq[:, 0:128]), [u8(T.vlq[:, 256 * k + 128 * o:256 * k + 128 * o + 128]) for k in range(3)],
+             s["va%d" % rank], s.sent)
+    n += cast(g, topo, core, cores, T.hs[:, 0:128], [T.vls[:, 256 * k + 128 * o:256 * k + 128 * o + 128] for k in range(3)],
+              s["va%d" % rank], s.sent)
+    g.wait_ge(s.sent, n)
+
+
+def rank_program(g, core, T, topo):
+    rank = T.rank_of(core)
+    if rank is None:
+        for r in range(len(T.cores)):
+            hs = helpers_of(r, T, topo)
+            if core in hs:
+                helper_program(g, core, T, topo, r, hs.index(core))
+        return
+    s = T.sem
+    peers = peers_of(rank, T, topo)
+    cores = [T.cores[r] for r in peers]
+    hs = helpers_of(rank, T, topo)
+    add, sub, mx, mn = AluOpType.add, AluOpType.subtract, AluOpType.max, AluOpType.min
+    act = ActivationFunctionType
+    v, a, t = g.vector, g.scalar, g.tensor
+
+    def load_qp(q, i):
+        q.dma_start(T.qpo[16 * i:16 * i + 16, :], T.qp[:, :]).then_inc(s.ldqp, 16)
+    g.sync.dma_start(T.xb[:, :], T.qx[:, :]).then_inc(s.ldx, 16)
+    for i in range(3):
+        load_qp(g.sync, i)
+    for i in range(3, 8):
+        load_qp(a, i)
+    g.sync.dma_start(T.vb[:, :], T.vv[:, :]).then_inc(s.ldv, 16)
+    a.dma_start(T.kpi[:, :], T.kp[:, :]).then_inc(s.ldkp, 16)
+    a.dma_start(T.rb[:, :], T.rt[:, :]).then_inc(s.ldr, 16)
+    g.sync.dma_start(T.kb[:, 0:1024], T.ky[:, 0:1024]).then_inc(s.ldk0, 16)
+    a.dma_start(T.kb[:, 1024:2048], T.ky[:, 1024:2048]).then_inc(s.ldk1, 16)
+
+    sent = 0
+    g.wait_ge(s.ldqp, 128)
+    sent += cast(g, topo, core, cores, T.qpo[:, 0:8], [T.qpl[:, 8 * k:8 * k + 8] for k in range(3)], s.qpa, s.sent)
+    g.wait_ge(s.qx, 1)
+    sent += cast(g, topo, core, cores, u8(T.xq[:, 0:128]), [u8(T.xlq[:, 128 * k:128 * k + 128]) for k in range(3)], s["xa%d" % rank], s.sent)
+    sent += cast(g, topo, core, cores, T.xs[:, 0:128], [T.xls[:, 128 * k:128 * k + 128] for k in range(3)], s["xa%d" % rank], s.sent)
+    off = topo.engines(core, cores[0])
+    on = [e for e in topo.engines(core, hs[0]) if e not in off]
+    half = len(on) // 2
+    masks = [bits(on[:half]), bits(on[half:])]
+    g.wait_ge(s.qv, 1)
+    for wide in (True, False):
+        tr = []
+        for o in range(2):
+            src, dst = (u8(T.vq[:, 128 * o:128 * o + 128]), u8(T.hq[:, 0:128])) if wide else (T.vs[:, 128 * o:128 * o + 128], T.hs[:, 0:128])
+            tr.append(RemoteDMATransfer(dst_ids=ids([hs[o]], topo), dma_engine_mask=masks[o], remote_sem=s.vh, srcs=[src], dsts=[dst], alu_op=0))
+        g.remote_dma_fused(tr, local_sem=s.sent)
+        sent += 2 * half
+    for k in range(3):
+        g.wait_ge(s["qa%d" % k], 1)
+        c = slice(128 * k, 128 * k + 128)
+        sent += cast(g, topo, core, [cores[k]], u8(T.aq[:, c]), [u8(T.alq[:, c])], s["aa%d" % rank], s.sent)
+        sent += cast(g, topo, core, [cores[k]], T.as_[:, c], [T.als[:, c]], s["aa%d" % rank], s.sent)
+    g.wait_ge(s.sent, sent)
+
+    def bank(i, n):
+        return T.ps[:, 512 * i:512 * i + n]
+
+    def kb(b):
+        return T.kq[:, 128 * b:128 * b + 128], T.ks[:, 128 * b:128 * b + 128]
+    t.wait_ge(s.qr, 1)
+    for b in range(4):
+        if b % 2 == 0:
+            t.wait_ge(s["qk%d" % (b // 2)], 1)
+        t.matmul_mx(bank(b, 256), *kb(b), T.rq[:, 0:256], T.rs[:, 0:256], True, True).then_inc(s["p%d" % b], 1)
+    first = [4, 0, 4, 0]
+    for k in range(4):
+        if k < 3:
+            t.wait_ge(s["xa%d" % peers[k]], 16)
+        else:
+            t.wait_ge(s.qx, 1)
+        for b in range(4):
+            if k == 1:
+                t.wait_ge(s["pc%d" % b], 1)
+            if k > 1:
+                t.wait_ge(s["ad%d%d" % (k - 2, b)], 1)
+            x = (T.xlq[:, 128 * k:128 * k + 128], T.xls[:, 128 * k:128 * k + 128]) if k < 3 else (T.xq[:, 0:128], T.xs[:, 0:128])
+            t.matmul_mx(bank(first[k] + b, 128), *kb(b), *x, True, True).then_inc(s["s%d%d" % (k, b)], 1)
+    for o in range(2):
+        t.wait_ge(s["ad2%d" % o], 1)
+    t.wait_ge(s.qv, 1)
+    t.wait_ge(s.qa3, 1)
+    for o in range(2):
+        w = slice(128 * o, 128 * o + 128)
+        t.matmul_mx(bank(4 + o, 128), T.vq[:, w], T.vs[:, w], T.aq[:, 384:512], T.as_[:, 384:512], True, False)
+    for k in range(3):
+        t.wait_ge(s["va%d" % peers[k]], 32)
+        t.wait_ge(s["aa%d" % peers[k]], 16)
+        for o in range(2):
+            w = slice(256 * k + 128 * o, 256 * k + 128 * o + 128)
+            c = slice(128 * k, 128 * k + 128)
+            m = t.matmul_mx(bank(4 + o, 128), T.vlq[:, w], T.vls[:, w], T.alq[:, c], T.als[:, c], False, k == 2)
+            if k == 2:
+                m.then_inc(s["y%d" % o], 1)
+
+    def quant(sem, q, sc, x, *waits):
+        for name, n in waits:
+            v.wait_ge(s[name], n)
+        v.quantize_mx(q, sc, x).then_inc(s[sem], 1)
+
+    def offsets(q, n, d, off, d1, done):
+        for b in range(4):
+            v.tensor_scalar(d[:, n * b:n * b + n], q, T.kpf[:, b:b + 1], -128.0, sub, mx).then_inc(s[d1], 1)
+        v.wait_ge(s[d1], 4)
+        v.tensor_scalar(off[:, 0:4 * n], d[:, 0:4 * n], 127.0, 128.0, mn, add).then_inc(s[done], 1)
+
+    def window(b):
+        return T.pw[:, 256 * b:256 * b + 256]
+
+    def picked(k, b):
+        return T.gr[:, 384 * b + 128 * k:384 * b + 128 * k + 128] if k < 3 else T.go[:, 128 * b:128 * b + 128]
+
+    def ublk(k, b):
+        return T.u[:, 512 * k + 128 * b:512 * k + 128 * b + 128]
+
+    def sums(k, bs):
+        for b in bs:
+            v.wait_ge(s[("g%d" if k < 3 else "go%d") % b], 1)
+            v.wait_ge(s["s%d%d" % (k, b)], 1)
+            v.tensor_tensor(ublk(k, b), bank(first[k] + b, 128), picked(k, b), add).then_inc(s["ad%d%d" % (k, b)], 1)
+
+    def quant_tile(k):
+        c = slice(128 * k, 128 * k + 128)
+        quant("qa%d" % k, T.aq[:, c], T.as_[:, c], T["h%d" % k][:, 0:512], ("rl%d" % k, 4))
+
+    quant("qx", T.xq[:, 0:128], T.xs[:, 0:128], T.xb[:, 0:512], ("ldx", 16))
+    v.wait_ge(s.ldkp, 16)
+    v.tensor_copy(T.kpf[:, 0:4], T.kpi[:, 0:4]).then_inc(s.kpf, 1)
+    v.wait_ge(s.kpf, 1)
+    v.wait_ge(s.ldqp, 128)
+    offsets(T.qpo[:, 0:8], 8, T.do, T.offo, "d1o", "offo")
+    quant("qv", T.vq[:, 0:256], T.vs[:, 0:256], T.vb[:, 0:1024], ("ldv", 16))
+    quant("qr", T.rq[:, 0:256], T.rs[:, 0:256], T.rb[:, 0:1024], ("ldr", 16))
+    for i in range(2):
+        c = slice(256 * i, 256 * i + 256)
+        quant("qk%d" % i, T.kq[:, c], T.ks[:, c], T.kb[:, 1024 * i:1024 * i + 1024], ("ldk%d" % i, 16))
+    v.wait_ge(s.qpa, 24)
+    offsets(T.qpl[:, 0:24], 24, T.dr, T.offr, "d1", "offr")
+    v.wait_ge(s.offr, 1)
+    for b in (0, 2):
+        v.wait_ge(s["pc%d" % b], 1)
+        v.tensor_copy(T.gr[:, 384 * b:384 * b + 384], window(b).indirect(T.offr[:, 24 * b:24 * b + 24])).then_inc(s["g%d" % b], 1)
+    sums(0, range(4))
+    sums(1, (0,))
+    quant_tile(0)
+    sums(1, (1, 2, 3))
+    sums(2, (0,))
+    quant_tile(1)
+    sums(2, (1, 2, 3))
+    quant_tile(2)
+    v.wait_ge(s.offo, 1)
+    for b in (0, 2):
+        v.tensor_copy(T.go[:, 128 * b:128 * b + 128], window(b).indirect(T.offo[:, 8 * b:8 * b + 8])).then_inc(s["go%d" % b], 1)
+    sums(3, range(4))
+    quant_tile(3)
+    v.wait_ge(s.y0, 1)
+    v.tensor_copy(T.yb[:, 0:128], bank(4, 128)).then_inc(s.yc, 1)
+
+    for b in range(4):
+        a.wait_ge(s["p%d" % b], 1)
+        a.activation(window(b), bank(b, 256), act.Copy).then_inc(s["pc%d" % b], 1)
+    a.wait_ge(s.offr, 1)
+    for b in (1, 3):
+        a.wait_ge(s["pc%d" % b], 1)
+        a.activation(T.gr[:, 384 * b:384 * b + 384], window(b).indirect(T.offr[:, 24 * b:24 * b + 24]), act.Copy).then_inc(s["g%d" % b], 1)
+
+    def relus(k):
+        for b in range(4):
+            a.wait_ge(s["ad%d%d" % (k, b)], 1)
+            a.activation(T["h%d" % k][:, b:512:4], ublk(k, b), act.Relu, scale=0.03125).then_inc(s["rl%d" % k], 1)
+    for k in range(3):
+        relus(k)
+    a.wait_ge(s.offo, 1)
+    for b in (1, 3):
+        a.activation(T.go[:, 128 * b:128 * b + 128], window(b).indirect(T.offo[:, 8 * b:8 * b + 8]), act.Copy).then_inc(s["go%d" % b], 1)
+    relus(3)
+    a.wait_ge(s.y1, 1)
+    a.activation(T.yb[:, 128:256], bank(5, 128), act.Copy).then_inc(s.yc, 1)
+
+    g.sync.wait_ge(s.yc, 2)
+    g.sync.dma_start(T.y[:, :], T.yb[:, :]).then_inc(s.st, 16)
+    g.sync.wait_ge(s.st, 16)

@@ -10,18 +10,22 @@ SCRATCH = {
     "rq": ("sbuf", [128, 256], C8), "rs": ("sbuf", [128, 256], U8), "vq": ("sbuf", [128, 256], C8), "vs": ("sbuf", [128, 256], U8),
     "qpl": ("sbuf", [128, 24], I32), "xlq": ("sbuf", [128, 384], C8), "xls": ("sbuf", [128, 384], U8),
     "vlq": ("sbuf", [128, 768], C8), "vls": ("sbuf", [128, 768], U8), "alq": ("sbuf", [128, 384], C8), "als": ("sbuf", [128, 384], U8),
-    "hq": ("sbuf", [128, 128], C8), "hs": ("sbuf", [128, 128], U8),
+    "hq": ("sbuf", [128, 128], C8),
     "dr": ("sbuf", [128, 96], F), "offr": ("sbuf", [128, 96], U16), "do": ("sbuf", [128, 32], F), "offo": ("sbuf", [128, 32], U16),
     "pw": ("sbuf", [128, 1024], F), "gr": ("sbuf", [128, 1536], F), "go": ("sbuf", [128, 512], F),
     "u": ("sbuf", [128, 2048], F), "h0": ("sbuf", [128, 512], B), "h1": ("sbuf", [128, 512], B), "h2": ("sbuf", [128, 512], B), "h3": ("sbuf", [128, 512], B),
-    "aq": ("sbuf", [128, 512], C8), "as_": ("sbuf", [128, 512], U8),
+    "aq": ("sbuf", [128, 512], C8), "asc": ("sbuf", [128, 512], U8),
     "yb": ("sbuf", [128, 256], F),
     "ps": ("psum", [128, 4096], F),
 }
 SEMAPHORES = (["ldx", "ldv", "ldr", "ldk0", "ldk1", "ldkp", "ldqp", "qx", "qv", "qr", "qk0", "qk1", "kpf", "d1", "d1o", "offr", "offo",
-               "qpa", "vh", "sent", "yc", "st"]
+               "qpa", "vh", "hkp", "hk0", "hk1", "sent", "yc", "st"]
               + [n + str(b) for n in ("p", "pc", "g", "go", "xa", "va", "aa", "rl", "qa") for b in range(4)]
               + [n + "%d%d" % (k, b) for n in ("s", "ad") for k in range(4) for b in range(4)] + ["y0", "y1"])
+ADD, SUB, MAX, MIN = AluOpType.add, AluOpType.subtract, AluOpType.max, AluOpType.min
+COPY, RELU = ActivationFunctionType.Copy, ActivationFunctionType.Relu
+TWIN = 2
+MINE = [k for k in range(3) if k != TWIN]
 
 
 def bits(engines):
@@ -37,10 +41,19 @@ def peers_of(rank, T, topo):
     return sorted((r for r in range(len(T.cores)) if r != rank), key=relation)
 
 
-def helpers_of(rank, T, topo):
+def free_writers(rank, T, topo, same_die):
     me = T.cores[rank]
     far = [T.cores[r] for r in range(len(T.cores)) if r != rank]
-    return [c for c in topo.cores_of(me) if topo.die(c) != topo.die(me) and all(topo.may_write(c, d) for d in far)][:2]
+    return [c for c in topo.cores_of(me)
+            if c != me and (topo.die(c) == topo.die(me)) == same_die and all(topo.may_write(c, d) for d in far)]
+
+
+def relays_of(rank, T, topo):
+    return free_writers(rank, T, topo, False)[:2]
+
+
+def twin_of(rank, T, topo):
+    return free_writers(rank, T, topo, True)[0]
 
 
 def ids(cores, topo):
@@ -48,10 +61,13 @@ def ids(cores, topo):
     return [DstId(rid=x[0], pnc=x[1]) for x in a]
 
 
-def cast(g, topo, src_core, cores, src, dsts, remote_sem, local_sem):
-    eng = [e for e in topo.engines(src_core, cores[0]) if all(e in topo.engines(src_core, c) for c in cores)]
-    g.remote_dma_fused([RemoteDMATransfer(dst_ids=ids(cores, topo), dma_engine_mask=bits(eng), remote_sem=remote_sem,
-                                          srcs=[src], dsts=dsts, alu_op=0)], local_sem=local_sem)
+def transfer(topo, cores, engines, src, dsts, sem):
+    return RemoteDMATransfer(dst_ids=ids(cores, topo), dma_engine_mask=bits(engines), remote_sem=sem, srcs=[src], dsts=dsts, alu_op=0)
+
+
+def cast(g, topo, me, cores, src, dsts, sem, local_sem):
+    eng = [e for e in topo.engines(me, cores[0]) if all(e in topo.engines(me, c) for c in cores)]
+    g.remote_dma_fused([transfer(topo, cores, eng, src, dsts, sem)], local_sem=local_sem)
     return len(eng)
 
 
@@ -59,14 +75,101 @@ def u8(v):
     return v.bitcast(dt.uint8)
 
 
-def helper_program(g, core, T, topo, rank, o):
+def cols(i, n=128):
+    return slice(n * i, n * i + n)
+
+
+def relay_program(g, core, T, topo, rank, o):
     s = T.sem
     cores = [T.cores[r] for r in peers_of(rank, T, topo)]
+    g.wait_ge(s.vh, 4)
+    n = cast(g, topo, core, cores, u8(T.hq[:, 0:128]), [u8(T.vlq[:, cols(2 * k + o)]) for k in range(3)], s["va%d" % rank], s.sent)
+    g.wait_ge(s.sent, n)
+
+
+def bank(T, i, n):
+    return T.ps[:, 512 * i:512 * i + n]
+
+
+def window(T, b):
+    return T.pw[:, cols(b, 256)]
+
+
+def kside(T, b):
+    return T.kq[:, cols(b)], T.ks[:, cols(b)]
+
+
+def offsets(v, T, q, n, d, off, d1, done):
+    s = T.sem
+    for b in range(4):
+        v.tensor_scalar(d[:, n * b:n * b + n], q, T.kpf[:, b:b + 1], -128.0, SUB, MAX).then_inc(s[d1], 1)
+    v.wait_ge(s[d1], 4)
+    v.tensor_scalar(off[:, 0:4 * n], d[:, 0:4 * n], 127.0, 128.0, MIN, ADD).then_inc(s[done], 1)
+
+
+def ublk(T, k, b):
+    return T.u[:, cols(4 * k + b)]
+
+
+def sums(v, T, k, bs, first, picked, gname):
+    s = T.sem
+    for b in bs:
+        v.wait_ge(s[gname % b], 1)
+        v.wait_ge(s["s%d%d" % (k, b)], 1)
+        v.tensor_tensor(ublk(T, k, b), bank(T, first + b, 128), picked(b), ADD).then_inc(s["ad%d%d" % (k, b)], 1)
+
+
+def relus(a, T, k):
+    s = T.sem
+    for b in range(4):
+        a.wait_ge(s["ad%d%d" % (k, b)], 1)
+        a.activation(T["h%d" % k][:, b:512:4], ublk(T, k, b), RELU, scale=0.03125).then_inc(s["rl%d" % k], 1)
+
+
+def quant_tile(v, T, k):
+    s = T.sem
+    v.wait_ge(s["rl%d" % k], 4)
+    v.quantize_mx(T.aq[:, cols(k)], T.asc[:, cols(k)], T["h%d" % k][:, 0:512]).then_inc(s["qa%d" % k], 1)
+
+
+def send_tile(g, T, topo, me, rank, k, to):
+    s = T.sem
+    g.wait_ge(s["qa%d" % k], 1)
+    n = cast(g, topo, me, [to], u8(T.aq[:, cols(k)]), [u8(T.alq[:, cols(k)])], s["aa%d" % rank], s.sent)
+    return n + cast(g, topo, me, [to], T.asc[:, cols(k)], [T.als[:, cols(k)]], s["aa%d" % rank], s.sent)
+
+
+def twin_program(g, core, T, topo, rank):
+    s, v, a, t = T.sem, g.vector, g.scalar, g.tensor
+    peers = peers_of(rank, T, topo)
+    k, peer = TWIN, peers[TWIN]
+    x = T.xlq[:, cols(k)], T.xls[:, cols(k)]
+    for b in range(4):
+        if b % 2 == 0:
+            t.wait_ge(s["hk%d" % (b // 2)], 16)
+        t.matmul_mx(bank(T, b, 256), *kside(T, b), T.rq[:, 0:256], T.rs[:, 0:256], True, True).then_inc(s["p%d" % b], 1)
+    t.wait_ge(s["xa%d" % peer], 16)
+    for b in range(4):
+        t.matmul_mx(bank(T, 4 + b, 128), *kside(T, b), *x, True, True).then_inc(s["s%d%d" % (k, b)], 1)
+    v.wait_ge(s.hkp, 8)
+    v.tensor_copy(T.kpf[:, 0:4], T.kpi[:, 0:4]).then_inc(s.kpf, 1)
+    v.wait_ge(s.kpf, 1)
+    v.wait_ge(s.qpa, 8)
+    offsets(v, T, T.qpl[:, 8 * k:8 * k + 8], 8, T.do, T.offo, "d1o", "offo")
+    a.wait_ge(s.offo, 1)
+    v.wait_ge(s.offo, 1)
+    for b in range(4):
+        q, copy = (v, v.tensor_copy) if b % 2 else (a, lambda o, i: a.activation(o, i, COPY))
+        q.wait_ge(s["p%d" % b], 1)
+        copy(window(T, b), bank(T, b, 256)).then_inc(s["pc%d" % b], 1)
+        q.wait_ge(s["pc%d" % b], 1)
+        copy(T.go[:, cols(b)], window(T, b).indirect(T.offo[:, cols(b, 8)])).then_inc(s["go%d" % b], 1)
+    sums(v, T, k, range(4), 4, lambda b: T.go[:, cols(b)], "go%d")
+    relus(a, T, k)
+    quant_tile(v, T, k)
     g.wait_ge(s.vh, 8)
-    n = cast(g, topo, core, cores, u8(T.hq[:, 0:128]), [u8(T.vlq[:, 256 * k + 128 * o:256 * k + 128 * o + 128]) for k in range(3)],
-             s["va%d" % rank], s.sent)
-    n += cast(g, topo, core, cores, T.hs[:, 0:128], [T.vls[:, 256 * k + 128 * o:256 * k + 128 * o + 128] for k in range(3)],
-              s["va%d" % rank], s.sent)
+    n = cast(g, topo, core, [T.cores[r] for r in peers], T.vs[:, 0:256], [T.vls[:, cols(i, 256)] for i in range(3)], s["va%d" % rank], s.sent)
+    n += send_tile(g, T, topo, core, rank, k, T.cores[peer])
     g.wait_ge(s.sent, n)
 
 
@@ -74,179 +177,149 @@ def rank_program(g, core, T, topo):
     rank = T.rank_of(core)
     if rank is None:
         for r in range(len(T.cores)):
-            hs = helpers_of(r, T, topo)
+            hs = relays_of(r, T, topo)
             if core in hs:
-                helper_program(g, core, T, topo, r, hs.index(core))
+                relay_program(g, core, T, topo, r, hs.index(core))
+            if core == twin_of(r, T, topo):
+                twin_program(g, core, T, topo, r)
         return
-    s = T.sem
+    s, v, a, t = T.sem, g.vector, g.scalar, g.tensor
     peers = peers_of(rank, T, topo)
     cores = [T.cores[r] for r in peers]
-    hs = helpers_of(rank, T, topo)
-    add, sub, mx, mn = AluOpType.add, AluOpType.subtract, AluOpType.max, AluOpType.min
-    act = ActivationFunctionType
-    v, a, t = g.vector, g.scalar, g.tensor
+    hs = relays_of(rank, T, topo)
+    twin = twin_of(rank, T, topo)
+    makers = [twin_of(r, T, topo) if k == TWIN else T.cores[r] for k, r in enumerate(peers)]
+    nm = len(MINE)
 
     def load_qp(q, i):
         q.dma_start(T.qpo[16 * i:16 * i + 16, :], T.qp[:, :]).then_inc(s.ldqp, 16)
     g.sync.dma_start(T.xb[:, :], T.qx[:, :]).then_inc(s.ldx, 16)
-    for i in range(3):
+    for i in range(4):
         load_qp(g.sync, i)
-    for i in range(3, 8):
-        load_qp(a, i)
-    g.sync.dma_start(T.vb[:, :], T.vv[:, :]).then_inc(s.ldv, 16)
+        load_qp(a, i + 4)
     a.dma_start(T.kpi[:, :], T.kp[:, :]).then_inc(s.ldkp, 16)
-    a.dma_start(T.rb[:, :], T.rt[:, :]).then_inc(s.ldr, 16)
-    g.sync.dma_start(T.kb[:, 0:1024], T.ky[:, 0:1024]).then_inc(s.ldk0, 16)
-    a.dma_start(T.kb[:, 1024:2048], T.ky[:, 1024:2048]).then_inc(s.ldk1, 16)
+    g.sync.dma_start(T.rb[:, :], T.rt[:, :]).then_inc(s.ldr, 16)
+    a.dma_start(T.kb[:, 0:1024], T.ky[:, 0:1024]).then_inc(s.ldk0, 16)
+    g.sync.dma_start(T.kb[:, 1024:2048], T.ky[:, 1024:2048]).then_inc(s.ldk1, 16)
+    a.dma_start(T.vb[:, :], T.vv[:, :]).then_inc(s.ldv, 16)
 
-    sent = 0
-    g.wait_ge(s.ldqp, 128)
-    sent += cast(g, topo, core, cores, T.qpo[:, 0:8], [T.qpl[:, 8 * k:8 * k + 8] for k in range(3)], s.qpa, s.sent)
-    g.wait_ge(s.qx, 1)
-    sent += cast(g, topo, core, cores, u8(T.xq[:, 0:128]), [u8(T.xlq[:, 128 * k:128 * k + 128]) for k in range(3)], s["xa%d" % rank], s.sent)
-    sent += cast(g, topo, core, cores, T.xs[:, 0:128], [T.xls[:, 128 * k:128 * k + 128] for k in range(3)], s["xa%d" % rank], s.sent)
     off = topo.engines(core, cores[0])
-    on = [e for e in topo.engines(core, hs[0]) if e not in off]
-    half = len(on) // 2
-    masks = [bits(on[:half]), bits(on[half:])]
+    on = [e for e in topo.engines(core, twin) if e not in off]
+    lo, hi = on[:len(on) // 2], on[len(on) // 2:]
+    sent = 0
+
+    def inside(sem, *transfers):
+        g.remote_dma_fused([transfer(topo, [c], e, src, [dst], sem) for c, e, src, dst in transfers], local_sem=s.sent)
+        return sum(len(x[1]) for x in transfers)
+    g.wait_ge(s.ldqp, 128)
+    sent += cast(g, topo, core, makers, T.qpo[:, 0:8], [T.qpl[:, cols(k, 8)] for k in range(3)], s.qpa, s.sent)
+    g.wait_ge(s.qx, 1)
+    sent += cast(g, topo, core, makers, u8(T.xq[:, 0:128]), [u8(T.xlq[:, cols(k)]) for k in range(3)], s["xa%d" % rank], s.sent)
+    sent += cast(g, topo, core, makers, T.xs[:, 0:128], [T.xls[:, cols(k)] for k in range(3)], s["xa%d" % rank], s.sent)
+    g.wait_ge(s.ldkp, 16)
+    sent += inside(s.hkp, (twin, on, T.kpi[:, 0:4], T.kpi[:, 0:4]))
+    g.wait_ge(s.qr, 1)
+    g.wait_ge(s.qk0, 1)
+    for x, c in ((u8(T.rq[:, 0:256]), u8(T.kq[:, 0:256])), (T.rs[:, 0:256], T.ks[:, 0:256])):
+        sent += inside(s.hk0, (twin, lo, x, x), (twin, hi, c, c))
+    g.wait_ge(s.qk1, 1)
+    for c in (u8(T.kq[:, 256:512]), T.ks[:, 256:512]):
+        sent += inside(s.hk1, (twin, off, c, c))
     g.wait_ge(s.qv, 1)
-    for wide in (True, False):
-        tr = []
-        for o in range(2):
-            src, dst = (u8(T.vq[:, 128 * o:128 * o + 128]), u8(T.hq[:, 0:128])) if wide else (T.vs[:, 128 * o:128 * o + 128], T.hs[:, 0:128])
-            tr.append(RemoteDMATransfer(dst_ids=ids([hs[o]], topo), dma_engine_mask=masks[o], remote_sem=s.vh, srcs=[src], dsts=[dst], alu_op=0))
-        g.remote_dma_fused(tr, local_sem=s.sent)
-        sent += 2 * half
-    for k in range(3):
-        g.wait_ge(s["qa%d" % k], 1)
-        c = slice(128 * k, 128 * k + 128)
-        sent += cast(g, topo, core, [cores[k]], u8(T.aq[:, c]), [u8(T.alq[:, c])], s["aa%d" % rank], s.sent)
-        sent += cast(g, topo, core, [cores[k]], T.as_[:, c], [T.als[:, c]], s["aa%d" % rank], s.sent)
+    sent += inside(s.vh, *((hs[o], (lo, hi)[o], u8(T.vq[:, cols(o)]), u8(T.hq[:, 0:128])) for o in range(2)))
+    sent += inside(s.vh, (twin, on, T.vs[:, 0:256], T.vs[:, 0:256]))
+    for k in MINE:
+        sent += send_tile(g, T, topo, core, rank, k, cores[k])
     g.wait_ge(s.sent, sent)
 
-    def bank(i, n):
-        return T.ps[:, 512 * i:512 * i + n]
-
-    def kb(b):
-        return T.kq[:, 128 * b:128 * b + 128], T.ks[:, 128 * b:128 * b + 128]
     t.wait_ge(s.qr, 1)
     for b in range(4):
         if b % 2 == 0:
             t.wait_ge(s["qk%d" % (b // 2)], 1)
-        t.matmul_mx(bank(b, 256), *kb(b), T.rq[:, 0:256], T.rs[:, 0:256], True, True).then_inc(s["p%d" % b], 1)
-    first = [4, 0, 4, 0]
-    for k in range(4):
-        if k < 3:
-            t.wait_ge(s["xa%d" % peers[k]], 16)
-        else:
+        t.matmul_mx(bank(T, b, 256), *kside(T, b), T.rq[:, 0:256], T.rs[:, 0:256], True, True).then_inc(s["p%d" % b], 1)
+    seq = MINE + [3]
+    first = {k: 4 - 4 * (i % 2) for i, k in enumerate(seq)}
+    for i, k in enumerate(seq):
+        if k == 3:
             t.wait_ge(s.qx, 1)
+            x = T.xq[:, 0:128], T.xs[:, 0:128]
+        else:
+            t.wait_ge(s["xa%d" % peers[k]], 16)
+            x = T.xlq[:, cols(k)], T.xls[:, cols(k)]
         for b in range(4):
-            if k == 1:
+            if i == 1:
                 t.wait_ge(s["pc%d" % b], 1)
-            if k > 1:
-                t.wait_ge(s["ad%d%d" % (k - 2, b)], 1)
-            x = (T.xlq[:, 128 * k:128 * k + 128], T.xls[:, 128 * k:128 * k + 128]) if k < 3 else (T.xq[:, 0:128], T.xs[:, 0:128])
-            t.matmul_mx(bank(first[k] + b, 128), *kb(b), *x, True, True).then_inc(s["s%d%d" % (k, b)], 1)
+            if i > 1:
+                t.wait_ge(s["ad%d%d" % (seq[i - 2], b)], 1)
+            t.matmul_mx(bank(T, first[k] + b, 128), *kside(T, b), *x, True, True).then_inc(s["s%d%d" % (k, b)], 1)
+    yb = first[seq[-2]]
     for o in range(2):
-        t.wait_ge(s["ad2%d" % o], 1)
+        t.wait_ge(s["ad%d%d" % (seq[-2], o)], 1)
     t.wait_ge(s.qv, 1)
     t.wait_ge(s.qa3, 1)
     for o in range(2):
-        w = slice(128 * o, 128 * o + 128)
-        t.matmul_mx(bank(4 + o, 128), T.vq[:, w], T.vs[:, w], T.aq[:, 384:512], T.as_[:, 384:512], True, False)
+        t.matmul_mx(bank(T, yb + o, 128), T.vq[:, cols(o)], T.vs[:, cols(o)], T.aq[:, cols(3)], T.asc[:, cols(3)], True, False)
     for k in range(3):
-        t.wait_ge(s["va%d" % peers[k]], 32)
+        t.wait_ge(s["va%d" % peers[k]], 24)
         t.wait_ge(s["aa%d" % peers[k]], 16)
         for o in range(2):
-            w = slice(256 * k + 128 * o, 256 * k + 128 * o + 128)
-            c = slice(128 * k, 128 * k + 128)
-            m = t.matmul_mx(bank(4 + o, 128), T.vlq[:, w], T.vls[:, w], T.alq[:, c], T.als[:, c], False, k == 2)
+            w = cols(2 * k + o)
+            m = t.matmul_mx(bank(T, yb + o, 128), T.vlq[:, w], T.vls[:, w], T.alq[:, cols(k)], T.als[:, cols(k)], False, k == 2)
             if k == 2:
                 m.then_inc(s["y%d" % o], 1)
 
-    def quant(sem, q, sc, x, *waits):
-        for name, n in waits:
-            v.wait_ge(s[name], n)
+    def quant(sem, q, sc, x, waited):
+        v.wait_ge(s[waited], 16)
         v.quantize_mx(q, sc, x).then_inc(s[sem], 1)
 
-    def offsets(q, n, d, off, d1, done):
-        for b in range(4):
-            v.tensor_scalar(d[:, n * b:n * b + n], q, T.kpf[:, b:b + 1], -128.0, sub, mx).then_inc(s[d1], 1)
-        v.wait_ge(s[d1], 4)
-        v.tensor_scalar(off[:, 0:4 * n], d[:, 0:4 * n], 127.0, 128.0, mn, add).then_inc(s[done], 1)
+    def picked(k):
+        return lambda b: T.gr[:, cols(nm * b + MINE.index(k))] if k < 3 else T.go[:, cols(b)]
 
-    def window(b):
-        return T.pw[:, 256 * b:256 * b + 256]
-
-    def picked(k, b):
-        return T.gr[:, 384 * b + 128 * k:384 * b + 128 * k + 128] if k < 3 else T.go[:, 128 * b:128 * b + 128]
-
-    def ublk(k, b):
-        return T.u[:, 512 * k + 128 * b:512 * k + 128 * b + 128]
-
-    def sums(k, bs):
-        for b in bs:
-            v.wait_ge(s[("g%d" if k < 3 else "go%d") % b], 1)
-            v.wait_ge(s["s%d%d" % (k, b)], 1)
-            v.tensor_tensor(ublk(k, b), bank(first[k] + b, 128), picked(k, b), add).then_inc(s["ad%d%d" % (k, b)], 1)
-
-    def quant_tile(k):
-        c = slice(128 * k, 128 * k + 128)
-        quant("qa%d" % k, T.aq[:, c], T.as_[:, c], T["h%d" % k][:, 0:512], ("rl%d" % k, 4))
-
-    quant("qx", T.xq[:, 0:128], T.xs[:, 0:128], T.xb[:, 0:512], ("ldx", 16))
+    quant("qx", T.xq[:, 0:128], T.xs[:, 0:128], T.xb[:, 0:512], "ldx")
+    quant("qr", T.rq[:, 0:256], T.rs[:, 0:256], T.rb[:, 0:1024], "ldr")
+    quant("qk0", T.kq[:, 0:256], T.ks[:, 0:256], T.kb[:, 0:1024], "ldk0")
     v.wait_ge(s.ldkp, 16)
     v.tensor_copy(T.kpf[:, 0:4], T.kpi[:, 0:4]).then_inc(s.kpf, 1)
+    quant("qk1", T.kq[:, 256:512], T.ks[:, 256:512], T.kb[:, 1024:2048], "ldk1")
+    quant("qv", T.vq[:, 0:256], T.vs[:, 0:256], T.vb[:, 0:1024], "ldv")
     v.wait_ge(s.kpf, 1)
-    v.wait_ge(s.ldqp, 128)
-    offsets(T.qpo[:, 0:8], 8, T.do, T.offo, "d1o", "offo")
-    quant("qv", T.vq[:, 0:256], T.vs[:, 0:256], T.vb[:, 0:1024], ("ldv", 16))
-    quant("qr", T.rq[:, 0:256], T.rs[:, 0:256], T.rb[:, 0:1024], ("ldr", 16))
-    for i in range(2):
-        c = slice(256 * i, 256 * i + 256)
-        quant("qk%d" % i, T.kq[:, c], T.ks[:, c], T.kb[:, 1024 * i:1024 * i + 1024], ("ldk%d" % i, 16))
-    v.wait_ge(s.qpa, 24)
-    offsets(T.qpl[:, 0:24], 24, T.dr, T.offr, "d1", "offr")
+    v.wait_ge(s.qpa, 8 * nm)
+    offsets(v, T, T.qpl[:, 0:8 * nm], 8 * nm, T.dr, T.offr, "d1", "offr")
     v.wait_ge(s.offr, 1)
     for b in (0, 2):
         v.wait_ge(s["pc%d" % b], 1)
-        v.tensor_copy(T.gr[:, 384 * b:384 * b + 384], window(b).indirect(T.offr[:, 24 * b:24 * b + 24])).then_inc(s["g%d" % b], 1)
-    sums(0, range(4))
-    sums(1, (0,))
-    quant_tile(0)
-    sums(1, (1, 2, 3))
-    sums(2, (0,))
-    quant_tile(1)
-    sums(2, (1, 2, 3))
-    quant_tile(2)
+        v.tensor_copy(T.gr[:, cols(b, 128 * nm)], window(T, b).indirect(T.offr[:, cols(b, 8 * nm)])).then_inc(s["g%d" % b], 1)
+    sums(v, T, MINE[0], range(4), first[MINE[0]], picked(MINE[0]), "g%d")
+    for k, nxt in zip(MINE, MINE[1:]):
+        sums(v, T, nxt, (0,), first[nxt], picked(nxt), "g%d")
+        quant_tile(v, T, k)
+        sums(v, T, nxt, (1, 2, 3), first[nxt], picked(nxt), "g%d")
+    v.wait_ge(s.ldqp, 128)
+    offsets(v, T, T.qpo[:, 0:8], 8, T.do, T.offo, "d1o", "offo")
+    quant_tile(v, T, MINE[-1])
     v.wait_ge(s.offo, 1)
     for b in (0, 2):
-        v.tensor_copy(T.go[:, 128 * b:128 * b + 128], window(b).indirect(T.offo[:, 8 * b:8 * b + 8])).then_inc(s["go%d" % b], 1)
-    sums(3, range(4))
-    quant_tile(3)
+        v.tensor_copy(T.go[:, cols(b)], window(T, b).indirect(T.offo[:, cols(b, 8)])).then_inc(s["go%d" % b], 1)
+    sums(v, T, 3, range(4), first[3], picked(3), "go%d")
+    quant_tile(v, T, 3)
     v.wait_ge(s.y0, 1)
-    v.tensor_copy(T.yb[:, 0:128], bank(4, 128)).then_inc(s.yc, 1)
+    v.tensor_copy(T.yb[:, 0:128], bank(T, yb, 128)).then_inc(s.yc, 1)
 
     for b in range(4):
         a.wait_ge(s["p%d" % b], 1)
-        a.activation(window(b), bank(b, 256), act.Copy).then_inc(s["pc%d" % b], 1)
+        a.activation(window(T, b), bank(T, b, 256), COPY).then_inc(s["pc%d" % b], 1)
     a.wait_ge(s.offr, 1)
     for b in (1, 3):
         a.wait_ge(s["pc%d" % b], 1)
-        a.activation(T.gr[:, 384 * b:384 * b + 384], window(b).indirect(T.offr[:, 24 * b:24 * b + 24]), act.Copy).then_inc(s["g%d" % b], 1)
-
-    def relus(k):
-        for b in range(4):
-            a.wait_ge(s["ad%d%d" % (k, b)], 1)
-            a.activation(T["h%d" % k][:, b:512:4], ublk(k, b), act.Relu, scale=0.03125).then_inc(s["rl%d" % k], 1)
-    for k in range(3):
-        relus(k)
+        a.activation(T.gr[:, cols(b, 128 * nm)], window(T, b).indirect(T.offr[:, cols(b, 8 * nm)]), COPY).then_inc(s["g%d" % b], 1)
+    for k in MINE:
+        relus(a, T, k)
     a.wait_ge(s.offo, 1)
     for b in (1, 3):
-        a.activation(T.go[:, 128 * b:128 * b + 128], window(b).indirect(T.offo[:, 8 * b:8 * b + 8]), act.Copy).then_inc(s["go%d" % b], 1)
-    relus(3)
+        a.activation(T.go[:, cols(b)], window(T, b).indirect(T.offo[:, cols(b, 8)]), COPY).then_inc(s["go%d" % b], 1)
+    relus(a, T, 3)
     a.wait_ge(s.y1, 1)
-    a.activation(T.yb[:, 128:256], bank(5, 128), act.Copy).then_inc(s.yc, 1)
+    a.activation(T.yb[:, 128:256], bank(T, yb + 1, 128), COPY).then_inc(s.yc, 1)
 
     g.sync.wait_ge(s.yc, 2)
     g.sync.dma_start(T.y[:, :], T.yb[:, :]).then_inc(s.st, 16)

from concourse.bass import DstId, RemoteDMATransfer
from concourse.mybir import dt, AluOpType, ActivationFunctionType

F, B, I32, U16 = "float32", "bfloat16", "int32", "uint16"
C8, U8 = "float8_e4m3fn_x4", "uint8"
SCRATCH = {
    "xb": ("sbuf", [128, 512], B), "kb": ("sbuf", [128, 2048], B), "rb": ("sbuf", [128, 1024], B), "vb": ("sbuf", [128, 1024], B),
    "kpi": ("sbuf", [128, 4], I32), "kpf": ("sbuf", [128, 4], F), "qpo": ("sbuf", [128, 8], I32),
    "xq": ("sbuf", [128, 128], C8), "xs": ("sbuf", [128, 128], U8), "kq": ("sbuf", [128, 512], C8), "ks": ("sbuf", [128, 512], U8),
    "rq": ("sbuf", [128, 256], C8), "rs": ("sbuf", [128, 256], U8), "vq": ("sbuf", [128, 256], C8), "vs": ("sbuf", [128, 256], U8),
    "qpl": ("sbuf", [128, 24], I32), "xlq": ("sbuf", [128, 384], C8), "xls": ("sbuf", [128, 384], U8),
    "vlq": ("sbuf", [128, 768], C8), "vls": ("sbuf", [128, 768], U8), "alq": ("sbuf", [128, 384], C8), "als": ("sbuf", [128, 384], U8),
    "hq": ("sbuf", [128, 128], C8),
    "dr": ("sbuf", [128, 96], F), "offr": ("sbuf", [128, 96], U16), "do": ("sbuf", [128, 32], F), "offo": ("sbuf", [128, 32], U16),
    "pw": ("sbuf", [128, 1024], F), "gr": ("sbuf", [128, 1536], F), "go": ("sbuf", [128, 512], F),
    "u": ("sbuf", [128, 2048], F), "h0": ("sbuf", [128, 512], B), "h1": ("sbuf", [128, 512], B), "h2": ("sbuf", [128, 512], B), "h3": ("sbuf", [128, 512], B),
    "aq": ("sbuf", [128, 512], C8), "asc": ("sbuf", [128, 512], U8),
    "yb": ("sbuf", [128, 256], F),
    "ps": ("psum", [128, 4096], F),
}
SEMAPHORES = (["ldx", "ldv", "ldr", "ldk0", "ldk1", "ldkp", "ldqp", "qx", "qv", "qr", "qk0", "qk1", "kpf", "d1", "d1o", "offr", "offo",
               "qpa", "vh", "hkp", "hk0", "hk1", "sent", "yc", "st"]
              + [n + str(b) for n in ("p", "pc", "g", "go", "xa", "va", "aa", "rl", "qa") for b in range(4)]
              + [n + "%d%d" % (k, b) for n in ("s", "ad") for k in range(4) for b in range(4)] + ["y0", "y1"])
ADD, SUB, MAX, MIN = AluOpType.add, AluOpType.subtract, AluOpType.max, AluOpType.min
COPY, RELU = ActivationFunctionType.Copy, ActivationFunctionType.Relu
TWIN = 2
MINE = [k for k in range(3) if k != TWIN]


def bits(engines):
    return sum(1 << e for e in engines)


def peers_of(rank, T, topo):
    me = topo.chip(T.cores[rank])

    def relation(r):
        c = topo.chip(T.cores[r])
        return 1 if topo.mates(me, c) else 2 if topo.same_plane(me, c) else 0
    return sorted((r for r in range(len(T.cores)) if r != rank), key=relation)


def free_writers(rank, T, topo, same_die):
    me = T.cores[rank]
    far = [T.cores[r] for r in range(len(T.cores)) if r != rank]
    return [c for c in topo.cores_of(me)
            if c != me and (topo.die(c) == topo.die(me)) == same_die and all(topo.may_write(c, d) for d in far)]


def relays_of(rank, T, topo):
    return free_writers(rank, T, topo, False)[:2]


def twin_of(rank, T, topo):
    return free_writers(rank, T, topo, True)[0]


def ids(cores, topo):
    a = [topo.addr(c) for c in cores]
    return [DstId(rid=x[0], pnc=x[1]) for x in a]


def transfer(topo, cores, engines, src, dsts, sem):
    return RemoteDMATransfer(dst_ids=ids(cores, topo), dma_engine_mask=bits(engines), remote_sem=sem, srcs=[src], dsts=dsts, alu_op=0)


def cast(g, topo, me, cores, src, dsts, sem, local_sem):
    eng = [e for e in topo.engines(me, cores[0]) if all(e in topo.engines(me, c) for c in cores)]
    g.remote_dma_fused([transfer(topo, cores, eng, src, dsts, sem)], local_sem=local_sem)
    return len(eng)


def u8(v):
    return v.bitcast(dt.uint8)


def cols(i, n=128):
    return slice(n * i, n * i + n)


def relay_program(g, core, T, topo, rank, o):
    s = T.sem
    cores = [T.cores[r] for r in peers_of(rank, T, topo)]
    g.wait_ge(s.vh, 4)
    n = cast(g, topo, core, cores, u8(T.hq[:, 0:128]), [u8(T.vlq[:, cols(2 * k + o)]) for k in range(3)], s["va%d" % rank], s.sent)
    g.wait_ge(s.sent, n)


def bank(T, i, n):
    return T.ps[:, 512 * i:512 * i + n]


def window(T, b):
    return T.pw[:, cols(b, 256)]


def kside(T, b):
    return T.kq[:, cols(b)], T.ks[:, cols(b)]


def offsets(v, T, q, n, d, off, d1, done):
    s = T.sem
    for b in range(4):
        v.tensor_scalar(d[:, n * b:n * b + n], q, T.kpf[:, b:b + 1], -128.0, SUB, MAX).then_inc(s[d1], 1)
    v.wait_ge(s[d1], 4)
    v.tensor_scalar(off[:, 0:4 * n], d[:, 0:4 * n], 127.0, 128.0, MIN, ADD).then_inc(s[done], 1)


def ublk(T, k, b):
    return T.u[:, cols(4 * k + b)]


def sums(v, T, k, bs, first, picked, gname):
    s = T.sem
    for b in bs:
        v.wait_ge(s[gname % b], 1)
        v.wait_ge(s["s%d%d" % (k, b)], 1)
        v.tensor_tensor(ublk(T, k, b), bank(T, first + b, 128), picked(b), ADD).then_inc(s["ad%d%d" % (k, b)], 1)


def relus(a, T, k):
    s = T.sem
    for b in range(4):
        a.wait_ge(s["ad%d%d" % (k, b)], 1)
        a.activation(T["h%d" % k][:, b:512:4], ublk(T, k, b), RELU, scale=0.03125).then_inc(s["rl%d" % k], 1)


def quant_tile(v, T, k):
    s = T.sem
    v.wait_ge(s["rl%d" % k], 4)
    v.quantize_mx(T.aq[:, cols(k)], T.asc[:, cols(k)], T["h%d" % k][:, 0:512]).then_inc(s["qa%d" % k], 1)


def send_tile(g, T, topo, me, rank, k, to):
    s = T.sem
    g.wait_ge(s["qa%d" % k], 1)
    n = cast(g, topo, me, [to], u8(T.aq[:, cols(k)]), [u8(T.alq[:, cols(k)])], s["aa%d" % rank], s.sent)
    return n + cast(g, topo, me, [to], T.asc[:, cols(k)], [T.als[:, cols(k)]], s["aa%d" % rank], s.sent)


def twin_program(g, core, T, topo, rank):
    s, v, a, t = T.sem, g.vector, g.scalar, g.tensor
    peers = peers_of(rank, T, topo)
    k, peer = TWIN, peers[TWIN]
    x = T.xlq[:, cols(k)], T.xls[:, cols(k)]
    for b in range(4):
        if b % 2 == 0:
            t.wait_ge(s["hk%d" % (b // 2)], 16)
        t.matmul_mx(bank(T, b, 256), *kside(T, b), T.rq[:, 0:256], T.rs[:, 0:256], True, True).then_inc(s["p%d" % b], 1)
    t.wait_ge(s["xa%d" % peer], 16)
    for b in range(4):
        t.matmul_mx(bank(T, 4 + b, 128), *kside(T, b), *x, True, True).then_inc(s["s%d%d" % (k, b)], 1)
    v.wait_ge(s.hkp, 8)
    v.tensor_copy(T.kpf[:, 0:4], T.kpi[:, 0:4]).then_inc(s.kpf, 1)
    v.wait_ge(s.kpf, 1)
    v.wait_ge(s.qpa, 8)
    offsets(v, T, T.qpl[:, 8 * k:8 * k + 8], 8, T.do, T.offo, "d1o", "offo")
    a.wait_ge(s.offo, 1)
    v.wait_ge(s.offo, 1)
    for b in range(4):
        q, copy = (v, v.tensor_copy) if b % 2 else (a, lambda o, i: a.activation(o, i, COPY))
        q.wait_ge(s["p%d" % b], 1)
        copy(window(T, b), bank(T, b, 256)).then_inc(s["pc%d" % b], 1)
        q.wait_ge(s["pc%d" % b], 1)
        copy(T.go[:, cols(b)], window(T, b).indirect(T.offo[:, cols(b, 8)])).then_inc(s["go%d" % b], 1)
    sums(v, T, k, range(4), 4, lambda b: T.go[:, cols(b)], "go%d")
    relus(a, T, k)
    quant_tile(v, T, k)
    g.wait_ge(s.vh, 8)
    n = cast(g, topo, core, [T.cores[r] for r in peers], T.vs[:, 0:256], [T.vls[:, cols(i, 256)] for i in range(3)], s["va%d" % rank], s.sent)
    n += send_tile(g, T, topo, core, rank, k, T.cores[peer])
    g.wait_ge(s.sent, n)


def rank_program(g, core, T, topo):
    rank = T.rank_of(core)
    if rank is None:
        for r in range(len(T.cores)):
            hs = relays_of(r, T, topo)
            if core in hs:
                relay_program(g, core, T, topo, r, hs.index(core))
            if core == twin_of(r, T, topo):
                twin_program(g, core, T, topo, r)
        return
    s, v, a, t = T.sem, g.vector, g.scalar, g.tensor
    peers = peers_of(rank, T, topo)
    cores = [T.cores[r] for r in peers]
    hs = relays_of(rank, T, topo)
    twin = twin_of(rank, T, topo)
    makers = [twin_of(r, T, topo) if k == TWIN else T.cores[r] for k, r in enumerate(peers)]
    nm = len(MINE)

    def load_qp(q, i):
        q.dma_start(T.qpo[16 * i:16 * i + 16, :], T.qp[:, :]).then_inc(s.ldqp, 16)
    g.sync.dma_start(T.xb[:, :], T.qx[:, :]).then_inc(s.ldx, 16)
    for i in range(4):
        load_qp(g.sync, i)
        load_qp(a, i + 4)
    a.dma_start(T.kpi[:, :], T.kp[:, :]).then_inc(s.ldkp, 16)
    g.sync.dma_start(T.rb[:, :], T.rt[:, :]).then_inc(s.ldr, 16)
    a.dma_start(T.kb[:, 0:1024], T.ky[:, 0:1024]).then_inc(s.ldk0, 16)
    g.sync.dma_start(T.kb[:, 1024:2048], T.ky[:, 1024:2048]).then_inc(s.ldk1, 16)
    a.dma_start(T.vb[:, :], T.vv[:, :]).then_inc(s.ldv, 16)

    off = topo.engines(core, cores[0])
    on = [e for e in topo.engines(core, twin) if e not in off]
    lo, hi = on[:len(on) // 2], on[len(on) // 2:]
    sent = 0

    def inside(sem, *transfers):
        g.remote_dma_fused([transfer(topo, [c], e, src, [dst], sem) for c, e, src, dst in transfers], local_sem=s.sent)
        return sum(len(x[1]) for x in transfers)
    g.wait_ge(s.ldqp, 128)
    sent += cast(g, topo, core, makers, T.qpo[:, 0:8], [T.qpl[:, cols(k, 8)] for k in range(3)], s.qpa, s.sent)
    g.wait_ge(s.qx, 1)
    sent += cast(g, topo, core, makers, u8(T.xq[:, 0:128]), [u8(T.xlq[:, cols(k)]) for k in range(3)], s["xa%d" % rank], s.sent)
    sent += cast(g, topo, core, makers, T.xs[:, 0:128], [T.xls[:, cols(k)] for k in range(3)], s["xa%d" % rank], s.sent)
    g.wait_ge(s.ldkp, 16)
    sent += inside(s.hkp, (twin, on, T.kpi[:, 0:4], T.kpi[:, 0:4]))
    g.wait_ge(s.qr, 1)
    g.wait_ge(s.qk0, 1)
    for x, c in ((u8(T.rq[:, 0:256]), u8(T.kq[:, 0:256])), (T.rs[:, 0:256], T.ks[:, 0:256])):
        sent += inside(s.hk0, (twin, lo, x, x), (twin, hi, c, c))
    g.wait_ge(s.qk1, 1)
    for c in (u8(T.kq[:, 256:512]), T.ks[:, 256:512]):
        sent += inside(s.hk1, (twin, off, c, c))
    g.wait_ge(s.qv, 1)
    sent += inside(s.vh, *((hs[o], (lo, hi)[o], u8(T.vq[:, cols(o)]), u8(T.hq[:, 0:128])) for o in range(2)))
    sent += inside(s.vh, (twin, on, T.vs[:, 0:256], T.vs[:, 0:256]))
    for k in MINE:
        sent += send_tile(g, T, topo, core, rank, k, cores[k])
    g.wait_ge(s.sent, sent)

    t.wait_ge(s.qr, 1)
    for b in range(4):
        if b % 2 == 0:
            t.wait_ge(s["qk%d" % (b // 2)], 1)
        t.matmul_mx(bank(T, b, 256), *kside(T, b), T.rq[:, 0:256], T.rs[:, 0:256], True, True).then_inc(s["p%d" % b], 1)
    seq = MINE + [3]
    first = {k: 4 - 4 * (i % 2) for i, k in enumerate(seq)}
    for i, k in enumerate(seq):
        if k == 3:
            t.wait_ge(s.qx, 1)
            x = T.xq[:, 0:128], T.xs[:, 0:128]
        else:
            t.wait_ge(s["xa%d" % peers[k]], 16)
            x = T.xlq[:, cols(k)], T.xls[:, cols(k)]
        for b in range(4):
            if i == 1:
                t.wait_ge(s["pc%d" % b], 1)
            if i > 1:
                t.wait_ge(s["ad%d%d" % (seq[i - 2], b)], 1)
            t.matmul_mx(bank(T, first[k] + b, 128), *kside(T, b), *x, True, True).then_inc(s["s%d%d" % (k, b)], 1)
    yb = first[seq[-2]]
    for o in range(2):
        t.wait_ge(s["ad%d%d" % (seq[-2], o)], 1)
    t.wait_ge(s.qv, 1)
    t.wait_ge(s.qa3, 1)
    for o in range(2):
        t.matmul_mx(bank(T, yb + o, 128), T.vq[:, cols(o)], T.vs[:, cols(o)], T.aq[:, cols(3)], T.asc[:, cols(3)], True, False)
    for k in range(3):
        t.wait_ge(s["va%d" % peers[k]], 24)
        t.wait_ge(s["aa%d" % peers[k]], 16)
        for o in range(2):
            w = cols(2 * k + o)
            m = t.matmul_mx(bank(T, yb + o, 128), T.vlq[:, w], T.vls[:, w], T.alq[:, cols(k)], T.als[:, cols(k)], False, k == 2)
            if k == 2:
                m.then_inc(s["y%d" % o], 1)

    def quant(sem, q, sc, x, waited):
        v.wait_ge(s[waited], 16)
        v.quantize_mx(q, sc, x).then_inc(s[sem], 1)

    def picked(k):
        return lambda b: T.gr[:, cols(nm * b + MINE.index(k))] if k < 3 else T.go[:, cols(b)]

    quant("qx", T.xq[:, 0:128], T.xs[:, 0:128], T.xb[:, 0:512], "ldx")
    quant("qr", T.rq[:, 0:256], T.rs[:, 0:256], T.rb[:, 0:1024], "ldr")
    quant("qk0", T.kq[:, 0:256], T.ks[:, 0:256], T.kb[:, 0:1024], "ldk0")
    v.wait_ge(s.ldkp, 16)
    v.tensor_copy(T.kpf[:, 0:4], T.kpi[:, 0:4]).then_inc(s.kpf, 1)
    quant("qk1", T.kq[:, 256:512], T.ks[:, 256:512], T.kb[:, 1024:2048], "ldk1")
    quant("qv", T.vq[:, 0:256], T.vs[:, 0:256], T.vb[:, 0:1024], "ldv")
    v.wait_ge(s.kpf, 1)
    v.wait_ge(s.qpa, 8 * nm)
    offsets(v, T, T.qpl[:, 0:8 * nm], 8 * nm, T.dr, T.offr, "d1", "offr")
    v.wait_ge(s.offr, 1)
    for b in (0, 2):
        v.wait_ge(s["pc%d" % b], 1)
        v.tensor_copy(T.gr[:, cols(b, 128 * nm)], window(T, b).indirect(T.offr[:, cols(b, 8 * nm)])).then_inc(s["g%d" % b], 1)
    sums(v, T, MINE[0], range(4), first[MINE[0]], picked(MINE[0]), "g%d")
    for k, nxt in zip(MINE, MINE[1:]):
        sums(v, T, nxt, (0,), first[nxt], picked(nxt), "g%d")
        quant_tile(v, T, k)
        sums(v, T, nxt, (1, 2, 3), first[nxt], picked(nxt), "g%d")
    v.wait_ge(s.ldqp, 128)
    offsets(v, T, T.qpo[:, 0:8], 8, T.do, T.offo, "d1o", "offo")
    quant_tile(v, T, MINE[-1])
    v.wait_ge(s.offo, 1)
    for b in (0, 2):
        v.tensor_copy(T.go[:, cols(b)], window(T, b).indirect(T.offo[:, cols(b, 8)])).then_inc(s["go%d" % b], 1)
    sums(v, T, 3, range(4), first[3], picked(3), "go%d")
    quant_tile(v, T, 3)
    v.wait_ge(s.y0, 1)
    v.tensor_copy(T.yb[:, 0:128], bank(T, yb, 128)).then_inc(s.yc, 1)

    for b in range(4):
        a.wait_ge(s["p%d" % b], 1)
        a.activation(window(T, b), bank(T, b, 256), COPY).then_inc(s["pc%d" % b], 1)
    a.wait_ge(s.offr, 1)
    for b in (1, 3):
        a.wait_ge(s["pc%d" % b], 1)
        a.activation(T.gr[:, cols(b, 128 * nm)], window(T, b).indirect(T.offr[:, cols(b, 8 * nm)]), COPY).then_inc(s["g%d" % b], 1)
    for k in MINE:
        relus(a, T, k)
    a.wait_ge(s.offo, 1)
    for b in (1, 3):
        a.activation(T.go[:, cols(b)], window(T, b).indirect(T.offo[:, cols(b, 8)]), COPY).then_inc(s["go%d" % b], 1)
    relus(a, T, 3)
    a.wait_ge(s.y1, 1)
    a.activation(T.yb[:, 128:256], bank(T, yb + 1, 128), COPY).then_inc(s.yc, 1)

    g.sync.wait_ge(s.yc, 2)
    g.sync.dma_start(T.y[:, :], T.yb[:, :]).then_inc(s.st, 16)
    g.sync.wait_ge(s.st, 16)
